import numpy as np
import ml_dtypes


def mxq(x, axis, fmt="e4m3"):
    dtype, down = {"e4m3": (ml_dtypes.float8_e4m3fn, 7), "e5m2": (ml_dtypes.float8_e5m2, 14)}[fmt]
    v = np.moveaxis(np.asarray(x, np.float32).astype(ml_dtypes.bfloat16).astype(np.float64), axis, -1)
    blocks = v.reshape(v.shape[:-1] + (-1, 32))
    amax = np.abs(blocks).max(-1, keepdims=True)
    byte = np.maximum(np.where(amax > 0, np.frexp(amax)[1] - 1 + 127, 0) - down, 1)
    scale = np.exp2(byte - 127.0)
    codes = (blocks / scale).astype(np.float32).astype(dtype).astype(np.float64)
    return np.moveaxis((codes * scale).reshape(v.shape), -1, axis)


WIDE = False


def mx_kscale(k):
    if not WIDE:
        return np.ones(k)
    levels = np.array([10, -10, 5, -5, 0])
    if k % 512:
        return np.exp2(np.random.permutation(np.resize(levels, k // 32))).repeat(32)
    a = np.empty((k // 512, 16))
    for p in range(k // 512):
        a[p, :8] = np.random.permutation(np.resize(levels, 8))
        for g in range(8):
            far = levels[np.abs(levels - a[p, g]) >= 10]
            a[p, g + 8] = far[np.random.randint(len(far))]
    return np.exp2(a.ravel()).repeat(32)


def f64(x):
    return np.asarray(x).astype(np.float64)


def striped(idx):
    return np.tile(np.asarray(idx).reshape(-1, 16).T, (8, 1)).astype(np.uint16)


def unstriped(offs):
    return offs[:16].T.reshape(-1).astype(np.int64)


E2M1 = np.array([0.0, 0.5, 1.0, 1.5, 2.0, 3.0, 4.0, 6.0, -0.0, -0.5, -1.0, -1.5, -2.0, -3.0, -4.0, -6.0])


def pack_weight(w, fmt):
    k, n = w.shape
    w = f64(np.asarray(w, np.float32).astype(ml_dtypes.bfloat16)).reshape(k // 32, 32, n)
    amax = np.abs(w).max(1)
    if fmt == "e4m3":
        byte = np.frexp(amax)[1] - 1 + 127 - 7
    else:
        mant, ex = np.frexp(amax / 6.0)
        byte = np.where(mant > 0.5, ex, ex - 1) + 127
    byte = np.clip(np.where(amax > 0, byte, 1), 1, 254)
    scaled = (w * np.exp2(127.0 - byte)[:, None, :]).reshape(k, n).astype(np.float32)
    by_word = np.ascontiguousarray(scaled.reshape(k // 512, 128, 4, n).transpose(0, 1, 3, 2))
    if fmt == "e4m3":
        words = by_word.astype(ml_dtypes.float8_e4m3fn).view(np.uint8)
    else:
        c = by_word.astype(ml_dtypes.float4_e2m1fn).view(np.uint8) & 0xF
        words = (c[..., 0::2] | (c[..., 1::2] << 4)).reshape(k // 512, 128, 2 * n)
    return np.ascontiguousarray(words), np.ascontiguousarray(byte.astype(np.uint8).reshape(k // 512, 16, n))


def unpack_weight(words, scales, fmt):
    g, _, n = scales.shape
    words = np.ascontiguousarray(words).reshape(g, 128, n, -1)
    if fmt == "e4m3":
        vals = words.view(ml_dtypes.float8_e4m3fn).astype(np.float64)
    else:
        nib = np.empty((g, 128, n, 4), np.uint8)
        nib[..., 0::2] = words & 0xF
        nib[..., 1::2] = words >> 4
        vals = E2M1[nib]
    vals = vals * np.repeat(np.exp2(scales.astype(np.float64) - 127.0), 8, axis=1)[..., None]
    return vals.transpose(0, 1, 3, 2).reshape(g * 512, n)


D, T, I, Q, E, Z, M, C = 512, 2048, 512, 256, 512, 1024, 1024, 512


def setup_inputs():
    n = np.random.standard_normal
    idx = np.random.permutation(T)[:I]
    idx2 = np.random.permutation(Z)[:I]
    idx3 = np.random.permutation(Z)[:I]
    idx4 = np.random.permutation(M)[:Q]
    fd = mx_kscale(D)
    fi = mx_kscale(I)
    fc = mx_kscale(C)
    ti = np.ones(T)
    ti[idx] = fi
    keysp = pack_weight(n((D, T)) / fd[:, None], "e4m3")
    return {
        "query": (n((D, Q)) * 1.0 / np.sqrt(D) * fd[:, None]).astype(np.float32),
        "keys_words": keysp[0],
        "keys_scales": keysp[1],
        "os": (np.random.uniform(0.02, 0.08, (1, I)) * fi).astype(np.float32),
        "vals": (n((E, T)) / ti).astype(np.float32),
        "wm": (n((C, E)) * 1.0 / np.sqrt(C) * fc[:, None]).astype(np.float32),
        "mstore": (n((C, M)) / fc[:, None]).astype(np.float32),
        "offs": striped(idx),
        "offs2": striped(idx2),
        "offs3": striped(idx3),
        "offs4": striped(idx4),
    }


def reference(query, keys_words, keys_scales, os, vals, wm, mstore, offs, offs2, offs3, offs4):
    idx = unstriped(offs)
    idx2 = unstriped(offs2)
    idx3 = unstriped(offs3)
    idx4 = unstriped(offs4)
    keysu = unpack_weight(keys_words, keys_scales, "e4m3")
    queryq = mxq(f64(query), 0, "e4m3")
    keysidxg = keysu[:, idx]
    a = queryq.T @ keysidxg
    f0 = np.zeros((Q, Z))
    f0[:, idx2] = a
    s = a + f0[:, idx3]
    w = np.maximum(s, 0.0)
    wo1 = w * f64(os)
    wt1 = wo1.T
    vt1 = f64(vals)[:, idx].T
    vt1q = mxq(vt1, 0, "e4m3")
    wt1q = mxq(wt1, 0, "e4m3")
    o = vt1q.T @ wt1q
    wmq = mxq(f64(wm), 0, "e4m3")
    mstoreq = mxq(f64(mstore), 0, "e4m3")
    me = wmq.T @ mstoreq
    y = np.maximum(o, me[:, idx4])
    return y

@@ -1,0 +1,197 @@
+from contextlib import ExitStack
+
+import concourse.mybir as mybir
+from concourse.masks import make_identity
+
+F32 = mybir.dt.float32
+BF16 = mybir.dt.bfloat16
+I32 = mybir.dt.int32
+U32 = mybir.dt.uint32
+U16 = mybir.dt.uint16
+U8 = mybir.dt.uint8
+FP8X4 = mybir.dt.float8_e4m3fn_x4
+COPY = mybir.ActivationFunctionType.Copy
+MAX = mybir.AluOpType.max
+MULT = mybir.AluOpType.mult
+ADD = mybir.AluOpType.add
+
+P = 128
+PACK = 4
+D, T, I, Q, E, Z, M, C = 512, 2048, 512, 256, 512, 1024, 1024, 512
+BANK = 512
+Q_TILES = Q // P
+E_TILES = E // P
+M_HALVES = M // BANK
+FLOPS = 2 * (D * I * Q + I * E * Q + C * E * M)
+
+
+def interleave_views(grouped, raw):
+    return (
+        grouped[:].rearrange("p (c i) t -> p c t i", i=4),
+        raw[:].rearrange("p t (c i) -> p c t i", i=4),
+    )
+
+
+def quantize(nc, codes, scales, grouped):
+    nc.vector.quantize_mx(out=codes.bitcast(FP8X4), scales=scales, in_=grouped)
+
+
+def tile_attend_passedthrough_memorylarger_lean_kernel(
+    tc, query, keys_words, keys_scales, slot_factor, vals, wm, mstore, offs, offs2, offs3, offs4, out
+):
+    nc = tc.nc
+    with ExitStack() as ctx:
+        sb = ctx.enter_context(tc.tile_pool(name="sb", bufs=1))
+        ps = ctx.enter_context(tc.psum_pool(name="ps", bufs=1))
+
+        def sbuf(name, shape, dtype, tag=None):
+            return sb.tile(shape, dtype, name=name, tag=tag or name, align_bytes=64)
+
+        def bank(name, shape, number):
+            return ps.tile(shape, F32, name=name, tag=f"bank{number}")
+
+        def product(out_ap, stationary, moving):
+            nc.tensor.matmul_mx(
+                out=out_ap,
+                lhsT=stationary[0].bitcast(FP8X4),
+                lhsT_scale=stationary[1],
+                rhs=moving[0].bitcast(FP8X4),
+                rhs_scale=moving[1],
+                start=True,
+                stop=True,
+            )
+
+        idx = sbuf("idx", [P, I // 16], U16)
+        idx2 = sbuf("idx2", [P, I // 16], U16)
+        idx3 = sbuf("idx3", [P, I // 16], U16)
+        idx4 = sbuf("idx4", [P, Q // 16], U16)
+        key_words = sbuf("key_words", [P, T], U32)
+        key_scales = sbuf("key_scales", [P, T], U8)
+        q_raw = sbuf("q_raw", [P, PACK, Q], F32)
+        wm_raw = sbuf("wm_raw", [P, PACK, E], F32)
+        ms_raw = [sbuf(f"ms_raw{h}", [P, PACK, BANK], F32, tag=f"ms_raw{h}") for h in range(M_HALVES)]
+        v_raw = [sbuf(f"v_raw{j}", [P, T], F32) for j in range(E_TILES)]
+        factor = sbuf("factor", [P, PACK], F32)
+        f0 = [sbuf(f"f0_{h}", [P, Z], F32) for h in range(Q_TILES)]
+        ident = sbuf("ident", [P, P], F32)
+
+        nc.vector.memset(key_scales[:].bitcast(I32), 0)
+        nc.sync.dma_start(idx[:], offs)
+        nc.sync.dma_start(
+            key_words[:].bitcast(I32), keys_words[0].rearrange("p n t -> p (n t)").bitcast(I32)
+        )
+        for quad in range(4):
+            nc.scalar.dma_start(
+                key_scales[32 * quad : 32 * quad + 4, :].bitcast(I32),
+                keys_scales[0, 4 * quad : 4 * quad + 4, :].bitcast(I32),
+            )
+        nc.sync.dma_start(q_raw[:], query.rearrange("(p t) q -> p t q", t=PACK))
+        nc.sync.dma_start(idx2[:], offs2)
+        nc.sync.dma_start(wm_raw[:], wm.rearrange("(p t) e -> p t e", t=PACK))
+        nc.sync.dma_start(idx3[:], offs3)
+        nc.sync.dma_start(idx4[:], offs4)
+        nc.sync.dma_start(factor[:], slot_factor.rearrange("o (p t) -> (o p) t", t=PACK))
+        ms_view = mstore.rearrange("(p t) m -> p t m", t=PACK)
+        for h in range(M_HALVES):
+            nc.sync.dma_start(ms_raw[h][:], ms_view[:, :, h * BANK : (h + 1) * BANK])
+        for j in range(E_TILES):
+            nc.sync.dma_start(v_raw[j][:], vals[j * P : (j + 1) * P, :])
+
+        for h in range(Q_TILES):
+            nc.vector.memset(f0[h][:], 0.0)
+        make_identity(nc, ident[:])
+
+        k_scales = sbuf("k_scales", [P, I], U8)
+        k_codes = sbuf("k_codes", [P, I], U32)
+        nc.vector.tensor_copy(k_scales[:], key_scales[:].indirect(idx[:]))
+        nc.vector.tensor_copy(k_codes[:], key_words[:].indirect(idx[:]))
+
+        q_grouped = sbuf("q_grouped", [P, Q, PACK], BF16)
+        q_codes = sbuf("q_codes", [P, Q], U32)
+        q_scales = sbuf("q_scales", [P, Q], U8)
+        dst, src = interleave_views(q_grouped, q_raw)
+        nc.scalar.activation(dst, src, COPY)
+        quantize(nc, q_codes[:], q_scales[:], q_grouped[:].rearrange("p q t -> p (q t)"))
+
+        a_sb = [sbuf(f"a_sb{h}", [P, I], F32) for h in range(Q_TILES)]
+        for h in range(Q_TILES):
+            a_ps = bank(f"a_ps{h}", [P, BANK], h)
+            cols = slice(h * P, (h + 1) * P)
+            product(a_ps[:], (q_codes[:, cols], q_scales[:, cols]), (k_codes[:], k_scales[:]))
+            nc.scalar.copy(a_sb[h][:], a_ps[:])
+
+        half = I // 2
+        for part in range(2):
+            for h in range(Q_TILES):
+                nc.scalar.activation(
+                    f0[h][:].indirect(idx2[:, part * (half // 16) : (part + 1) * (half // 16)]),
+                    a_sb[h][:, part * half : (part + 1) * half],
+                    COPY,
+                )
+
+        wm_grouped = sbuf("wm_grouped", [P, E, PACK], BF16)
+        wm_codes = sbuf("wm_codes", [P, E], U32)
+        wm_scales = sbuf("wm_scales", [P, E], U8)
+        dst, src = interleave_views(wm_grouped, wm_raw)
+        nc.vector.tensor_copy(dst, src)
+        quantize(nc, wm_codes[:], wm_scales[:], wm_grouped[:].rearrange("p e t -> p (e t)"))
+
+        me = [sbuf(f"me{j}", [P, M], F32) for j in range(E_TILES)]
+        me_ps = []
+        for h in range(M_HALVES):
+            ms_grouped = sbuf(f"ms_grouped{h}", [P, BANK, PACK], BF16)
+            ms_codes = sbuf(f"ms_codes{h}", [P, BANK], U32)
+            ms_scales = sbuf(f"ms_scales{h}", [P, BANK], U8)
+            dst, src = interleave_views(ms_grouped, ms_raw[h])
+            nc.vector.tensor_copy(dst, src)
+            quantize(nc, ms_codes[:], ms_scales[:], ms_grouped[:].rearrange("p m t -> p (m t)"))
+            for j in range(E_TILES):
+                me_bank = bank(f"me_ps{h}{j}", [P, BANK], (2 + E_TILES * h + j) % 8)
+                cols = slice(j * P, (j + 1) * P)
+                product(me_bank[:], (wm_codes[:, cols], wm_scales[:, cols]), (ms_codes[:], ms_scales[:]))
+                me_ps.append(me_bank)
+        for j in range(E_TILES):
+            nc.scalar.copy(me[j][:, 0:BANK], me_ps[j][:])
+
+        w_grouped = sbuf("w_grouped", [P, Q, PACK], BF16)
+        w_codes = sbuf("w_codes", [P, Q], U32)
+        w_scales = sbuf("w_scales", [P, Q], U8)
+        s_turned = []
+        for h in range(Q_TILES):
+            s_sb = sbuf(f"s_sb{h}", [P, I], F32, tag=("ms_raw1", "ms_grouped1")[h])
+            nc.vector.tensor_tensor(s_sb[:], f0[h][:].indirect(idx3[:]), a_sb[h][:], ADD)
+            s_turned.append(bank(f"s_turned{h}", [P, PACK, P], 2 + h))
+            for t in range(PACK):
+                nc.tensor.transpose(s_turned[h][:, t, :], s_sb[:, t::PACK], ident[:])
+        for j in range(E_TILES):
+            nc.vector.tensor_copy(me[j][:, BANK:M], me_ps[E_TILES + j][:])
+        for h in range(Q_TILES):
+            nc.vector.scalar_tensor_tensor(
+                out=w_grouped[:, h * P : (h + 1) * P, :],
+                in0=s_turned[h][:].rearrange("p t q -> p q t"),
+                scalar=0.0,
+                in1=factor[:].unsqueeze(1).to_broadcast([P, P, PACK]),
+                op0=MAX,
+                op1=MULT,
+            )
+        quantize(nc, w_codes[:], w_scales[:], w_grouped[:].rearrange("p q t -> p (q t)"))
+
+        for j in range(E_TILES):
+            me_listed = sbuf(f"me_listed{j}", [P, Q], F32)
+            nc.vector.tensor_copy(me_listed[:], me[j][:].indirect(idx4[:]))
+            v_listed = sbuf(f"v_listed{j}", [P, I], BF16, tag="ms_grouped1" if j == 0 else None)
+            nc.scalar.activation(v_listed[:], v_raw[j][:].indirect(idx[:]), COPY)
+            pairs = v_listed[:].bitcast(F32)
+            v_turned = bank(f"v_turned{j}", [P, 2, P], (4, 5, 2, 3)[j])
+            for u in range(2):
+                nc.tensor.transpose(v_turned[:, u, :], pairs[:, u::2], ident[:])
+            v_grouped = sbuf(f"v_grouped{j}", [P, P, 2], F32)
+            nc.scalar.copy(v_grouped[:], v_turned[:].rearrange("p u e -> p e u"))
+            v_codes = sbuf(f"v_codes{j}", [P, P], U32)
+            v_scales = sbuf(f"v_scales{j}", [P, P], U8)
+            quantize(nc, v_codes[:], v_scales[:], v_grouped[:].rearrange("p e u -> p (e u)").bitcast(BF16))
+            o_bank = bank(f"o_bank{j}", [P, Q], (6 + j) % 8)
+            product(o_bank[:], (v_codes[:], v_scales[:]), (w_codes[:], w_scales[:]))
+            result = sbuf(f"result{j}", [P, Q], F32)
+            nc.vector.tensor_tensor(result[:], o_bank[:], me_listed[:], MAX)
+            nc.sync.dma_start(out[j * P : (j + 1) * P, :], result[:])

@@ -27,8 +27,8 @@ FLOPS = 2 * (D * I * Q + I * E * Q + C * E * M)
 
 def interleave_views(grouped, raw):
     return (
-        grouped[:].rearrange("p (c i) t -> p c t i", i=4),
-        raw[:].rearrange("p t (c i) -> p c t i", i=4),
+        grouped.rearrange("p (c i) t -> p c t i", i=4),
+        raw.rearrange("p t (c i) -> p c t i", i=4),
     )
 
 
@@ -101,50 +101,61 @@ def tile_attend_passedthrough_memorylarger_lean_kernel(
             nc.vector.memset(f0[h][:], 0.0)
         make_identity(nc, ident[:])
 
-        k_scales = sbuf("k_scales", [P, I], U8)
-        k_codes = sbuf("k_codes", [P, I], U32)
-        nc.vector.tensor_copy(k_scales[:], key_scales[:].indirect(idx[:]))
-        nc.vector.tensor_copy(k_codes[:], key_words[:].indirect(idx[:]))
-
-        q_grouped = sbuf("q_grouped", [P, Q, PACK], BF16)
-        q_codes = sbuf("q_codes", [P, Q], U32)
-        q_scales = sbuf("q_scales", [P, Q], U8)
-        dst, src = interleave_views(q_grouped, q_raw)
-        nc.scalar.activation(dst, src, COPY)
-        quantize(nc, q_codes[:], q_scales[:], q_grouped[:].rearrange("p q t -> p (q t)"))
-
-        a_sb = [sbuf(f"a_sb{h}", [P, I], F32) for h in range(Q_TILES)]
-        for h in range(Q_TILES):
-            a_ps = bank(f"a_ps{h}", [P, BANK], h)
-            cols = slice(h * P, (h + 1) * P)
-            product(a_ps[:], (q_codes[:, cols], q_scales[:, cols]), (k_codes[:], k_scales[:]))
-            nc.scalar.copy(a_sb[h][:], a_ps[:])
-
         half = I // 2
-        for part in range(2):
-            for h in range(Q_TILES):
-                nc.scalar.activation(
-                    f0[h][:].indirect(idx2[:, part * (half // 16) : (part + 1) * (half // 16)]),
-                    a_sb[h][:, part * half : (part + 1) * half],
-                    COPY,
-                )
 
-        wm_grouped = sbuf("wm_grouped", [P, E, PACK], BF16)
-        wm_codes = sbuf("wm_codes", [P, E], U32)
-        wm_scales = sbuf("wm_scales", [P, E], U8)
-        dst, src = interleave_views(wm_grouped, wm_raw)
-        nc.vector.tensor_copy(dst, src)
-        quantize(nc, wm_codes[:], wm_scales[:], wm_grouped[:].rearrange("p e t -> p (e t)"))
+        def list_half(offsets, part):
+            return offsets[:, part * (half // 16) : (part + 1) * (half // 16)]
+
+        k_scales = sbuf("k_scales", [P, I], U8)
+        k_codes = [None, None]
+        k_codes[0] = sbuf("k_codes0", [P, half], U32)
+        nc.vector.tensor_copy(k_codes[0][:], key_words[:].indirect(list_half(idx, 0)))
+        nc.vector.tensor_copy(k_scales[:], key_scales[:].indirect(idx[:]))
+
+        q_mx = []
+        for h in range(Q_TILES):
+            q_grouped = sbuf(f"q_grouped{h}", [P, P, PACK], BF16)
+            q_codes = sbuf(f"q_codes{h}", [P, P], U32)
+            q_scales = sbuf(f"q_scales{h}", [P, P], U8)
+            dst, src = interleave_views(q_grouped[:], q_raw[:, :, h * P : (h + 1) * P])
+            nc.scalar.activation(dst, src, COPY)
+            quantize(nc, q_codes[:], q_scales[:], q_grouped[:].rearrange("p q t -> p (q t)"))
+            q_mx.append((q_codes[:], q_scales[:]))
+        k_codes[1] = sbuf("k_codes1", [P, half], U32, tag="q_grouped1")
+        nc.vector.tensor_copy(k_codes[1][:], key_words[:].indirect(list_half(idx, 1)))
+
+        a_sb = sbuf("a_sb", [P, Q_TILES, I], F32)
+        for h in range(Q_TILES):
+            a_first = bank(f"a_first{h}", [P, half], h)
+            product(a_first[:], q_mx[h], (k_codes[0][:], k_scales[:, 0:half]))
+            nc.scalar.copy(a_sb[:, h, 0:half], a_first[:])
+            nc.scalar.activation(f0[h][:].indirect(list_half(idx2, 0)), a_sb[:, h, 0:half], COPY)
+        a_second = bank("a_second", [P, Q_TILES, half], 1)
+        for h in range(Q_TILES):
+            product(a_second[:, h, :], q_mx[h], (k_codes[1][:], k_scales[:, half:I]))
+        for h in range(Q_TILES):
+            nc.scalar.copy(a_sb[:, h, half:I], a_second[:, h, :])
+            nc.scalar.activation(f0[h][:].indirect(list_half(idx2, 1)), a_sb[:, h, half:I], COPY)
+
+        def round_and_quantize(name, raw):
+            width = raw.shape[2]
+            grouped = sbuf(f"{name}_grouped", [P, width, PACK], BF16)
+            codes = sbuf(f"{name}_codes", [P, width], U32)
+            scales = sbuf(f"{name}_scales", [P, width], U8)
+            pieces = [slice(0, width // 2), slice(width // 2, width)]
+            for cols in pieces:
+                dst, src = interleave_views(grouped[:, cols, :], raw[:, :, cols])
+                nc.vector.tensor_copy(dst, src)
+            for cols in pieces:
+                quantize(nc, codes[:, cols], scales[:, cols], grouped[:, cols, :].rearrange("p c t -> p (c t)"))
+            return codes, scales
+
+        wm_codes, wm_scales = round_and_quantize("wm", wm_raw)
 
         me = [sbuf(f"me{j}", [P, M], F32) for j in range(E_TILES)]
         me_ps = []
         for h in range(M_HALVES):
-            ms_grouped = sbuf(f"ms_grouped{h}", [P, BANK, PACK], BF16)
-            ms_codes = sbuf(f"ms_codes{h}", [P, BANK], U32)
-            ms_scales = sbuf(f"ms_scales{h}", [P, BANK], U8)
-            dst, src = interleave_views(ms_grouped, ms_raw[h])
-            nc.vector.tensor_copy(dst, src)
-            quantize(nc, ms_codes[:], ms_scales[:], ms_grouped[:].rearrange("p m t -> p (m t)"))
+            ms_codes, ms_scales = round_and_quantize(f"ms{h}", ms_raw[h])
             for j in range(E_TILES):
                 me_bank = bank(f"me_ps{h}{j}", [P, BANK], (2 + E_TILES * h + j) % 8)
                 cols = slice(j * P, (j + 1) * P)
@@ -156,13 +167,13 @@ def tile_attend_passedthrough_memorylarger_lean_kernel(
         w_grouped = sbuf("w_grouped", [P, Q, PACK], BF16)
         w_codes = sbuf("w_codes", [P, Q], U32)
         w_scales = sbuf("w_scales", [P, Q], U8)
+        s_sb = sbuf("s_sb", [P, Q_TILES, I], F32, tag="ms1_grouped")
         s_turned = []
         for h in range(Q_TILES):
-            s_sb = sbuf(f"s_sb{h}", [P, I], F32, tag=("ms_raw1", "ms_grouped1")[h])
-            nc.vector.tensor_tensor(s_sb[:], f0[h][:].indirect(idx3[:]), a_sb[h][:], ADD)
+            nc.vector.tensor_tensor(s_sb[:, h, :], f0[h][:].indirect(idx3[:]), a_sb[:, h, :], ADD)
             s_turned.append(bank(f"s_turned{h}", [P, PACK, P], 2 + h))
             for t in range(PACK):
-                nc.tensor.transpose(s_turned[h][:, t, :], s_sb[:, t::PACK], ident[:])
+                nc.tensor.transpose(s_turned[h][:, t, :], s_sb[:, h, t::PACK], ident[:])
         for j in range(E_TILES):
             nc.vector.tensor_copy(me[j][:, BANK:M], me_ps[E_TILES + j][:])
         for h in range(Q_TILES):
@@ -176,22 +187,23 @@ def tile_attend_passedthrough_memorylarger_lean_kernel(
             )
         quantize(nc, w_codes[:], w_scales[:], w_grouped[:].rearrange("p q t -> p (q t)"))
 
+
         for j in range(E_TILES):
-            me_listed = sbuf(f"me_listed{j}", [P, Q], F32)
-            nc.vector.tensor_copy(me_listed[:], me[j][:].indirect(idx4[:]))
-            v_listed = sbuf(f"v_listed{j}", [P, I], BF16, tag="ms_grouped1" if j == 0 else None)
+            v_listed = sbuf(f"v_listed{j}", [P, I], BF16)
             nc.scalar.activation(v_listed[:], v_raw[j][:].indirect(idx[:]), COPY)
             pairs = v_listed[:].bitcast(F32)
-            v_turned = bank(f"v_turned{j}", [P, 2, P], (4, 5, 2, 3)[j])
+            v_turned = bank(f"v_turned{j}", [P, 2, P], 4 + j)
             for u in range(2):
                 nc.tensor.transpose(v_turned[:, u, :], pairs[:, u::2], ident[:])
-            v_grouped = sbuf(f"v_grouped{j}", [P, P, 2], F32)
+            v_grouped = sbuf(f"v_grouped{j}", [P, P, 2], F32, tag=f"v_raw{j + 1}")
             nc.scalar.copy(v_grouped[:], v_turned[:].rearrange("p u e -> p e u"))
             v_codes = sbuf(f"v_codes{j}", [P, P], U32)
             v_scales = sbuf(f"v_scales{j}", [P, P], U8)
             quantize(nc, v_codes[:], v_scales[:], v_grouped[:].rearrange("p e u -> p (e u)").bitcast(BF16))
-            o_bank = bank(f"o_bank{j}", [P, Q], (6 + j) % 8)
+            o_bank = bank(f"o_bank{j}", [P, Q], j)
             product(o_bank[:], (v_codes[:], v_scales[:]), (w_codes[:], w_scales[:]))
+            me_listed = sbuf(f"me_listed{j}", [P, Q], F32)
+            nc.vector.tensor_copy(me_listed[:], me[j][:].indirect(idx4[:]))
             result = sbuf(f"result{j}", [P, Q], F32)
             nc.vector.tensor_tensor(result[:], o_bank[:], me_listed[:], MAX)
             nc.sync.dma_start(out[j * P : (j + 1) * P, :], result[:])

@@ -75,17 +75,17 @@ def tile_attend_passedthrough_memorylarger_lean_kernel(
         f0 = [sbuf(f"f0_{h}", [P, Z], F32) for h in range(Q_TILES)]
         ident = sbuf("ident", [P, P], F32)
 
-        nc.vector.memset(key_scales[:].bitcast(I32), 0)
+        nc.gpsimd.memset(key_scales[:].bitcast(I32), 0)
+        nc.sync.dma_start(q_raw[:], query.rearrange("(p t) q -> p t q", t=PACK))
         nc.sync.dma_start(idx[:], offs)
-        nc.sync.dma_start(
-            key_words[:].bitcast(I32), keys_words[0].rearrange("p n t -> p (n t)").bitcast(I32)
-        )
         for quad in range(4):
-            nc.scalar.dma_start(
+            nc.sync.dma_start(
                 key_scales[32 * quad : 32 * quad + 4, :].bitcast(I32),
                 keys_scales[0, 4 * quad : 4 * quad + 4, :].bitcast(I32),
             )
-        nc.sync.dma_start(q_raw[:], query.rearrange("(p t) q -> p t q", t=PACK))
+        nc.sync.dma_start(
+            key_words[:].bitcast(I32), keys_words[0].rearrange("p n t -> p (n t)").bitcast(I32)
+        )
         nc.sync.dma_start(idx2[:], offs2)
         nc.sync.dma_start(wm_raw[:], wm.rearrange("(p t) e -> p t e", t=PACK))
         nc.sync.dma_start(idx3[:], offs3)
@@ -107,10 +107,10 @@ def tile_attend_passedthrough_memorylarger_lean_kernel(
             return offsets[:, part * (half // 16) : (part + 1) * (half // 16)]
 
         k_scales = sbuf("k_scales", [P, I], U8)
+        nc.vector.tensor_copy(k_scales[:], key_scales[:].indirect(idx[:]))
         k_codes = [None, None]
         k_codes[0] = sbuf("k_codes0", [P, half], U32)
         nc.vector.tensor_copy(k_codes[0][:], key_words[:].indirect(list_half(idx, 0)))
-        nc.vector.tensor_copy(k_scales[:], key_scales[:].indirect(idx[:]))
 
         q_mx = []
         for h in range(Q_TILES):
@@ -121,14 +121,17 @@ def tile_attend_passedthrough_memorylarger_lean_kernel(
             nc.scalar.activation(dst, src, COPY)
             quantize(nc, q_codes[:], q_scales[:], q_grouped[:].rearrange("p q t -> p (q t)"))
             q_mx.append((q_codes[:], q_scales[:]))
-        k_codes[1] = sbuf("k_codes1", [P, half], U32, tag="q_grouped1")
+        k_codes[1] = sbuf("k_codes1", [P, half], U32)
         nc.vector.tensor_copy(k_codes[1][:], key_words[:].indirect(list_half(idx, 1)))
 
         a_sb = sbuf("a_sb", [P, Q_TILES, I], F32)
         for h in range(Q_TILES):
             a_first = bank(f"a_first{h}", [P, half], h)
             product(a_first[:], q_mx[h], (k_codes[0][:], k_scales[:, 0:half]))
-            nc.scalar.copy(a_sb[:, h, 0:half], a_first[:])
+            if h == 0:
+                nc.scalar.copy(a_sb[:, h, 0:half], a_first[:])
+            else:
+                nc.vector.tensor_copy(a_sb[:, h, 0:half], a_first[:])
             nc.scalar.activation(f0[h][:].indirect(list_half(idx2, 0)), a_sb[:, h, 0:half], COPY)
         a_second = bank("a_second", [P, Q_TILES, half], 1)
         for h in range(Q_TILES):
@@ -188,6 +191,8 @@ def tile_attend_passedthrough_memorylarger_lean_kernel(
         quantize(nc, w_codes[:], w_scales[:], w_grouped[:].rearrange("p q t -> p (q t)"))
 
 
+        last = E_TILES - 1
+        last_listed = None
         for j in range(E_TILES):
             v_listed = sbuf(f"v_listed{j}", [P, I], BF16)
             nc.scalar.activation(v_listed[:], v_raw[j][:].indirect(idx[:]), COPY)
@@ -195,15 +200,22 @@ def tile_attend_passedthrough_memorylarger_lean_kernel(
             v_turned = bank(f"v_turned{j}", [P, 2, P], 4 + j)
             for u in range(2):
                 nc.tensor.transpose(v_turned[:, u, :], pairs[:, u::2], ident[:])
-            v_grouped = sbuf(f"v_grouped{j}", [P, P, 2], F32, tag=f"v_raw{j + 1}")
-            nc.scalar.copy(v_grouped[:], v_turned[:].rearrange("p u e -> p e u"))
+            staged = sbuf(f"staged{j}", [P, 2 * P + (Q if j == last - 1 else 0)], F32, tag=f"v_raw{j + 1}")
+            v_grouped = staged[:, 0 : 2 * P]
+            if j == last - 1:
+                last_listed = staged[:, 2 * P :]
+            nc.scalar.copy(v_grouped.rearrange("p (e u) -> p e u", u=2), v_turned[:].rearrange("p u e -> p e u"))
             v_codes = sbuf(f"v_codes{j}", [P, P], U32)
             v_scales = sbuf(f"v_scales{j}", [P, P], U8)
-            quantize(nc, v_codes[:], v_scales[:], v_grouped[:].rearrange("p e u -> p (e u)").bitcast(BF16))
+            quantize(nc, v_codes[:], v_scales[:], v_grouped.bitcast(BF16))
             o_bank = bank(f"o_bank{j}", [P, Q], j)
             product(o_bank[:], (v_codes[:], v_scales[:]), (w_codes[:], w_scales[:]))
-            me_listed = sbuf(f"me_listed{j}", [P, Q], F32)
-            nc.vector.tensor_copy(me_listed[:], me[j][:].indirect(idx4[:]))
+            if j == last:
+                me_listed = last_listed
+                nc.scalar.activation(me_listed, me[j][:].indirect(idx4[:]), COPY)
+            else:
+                me_listed = sbuf(f"me_listed{j}", [P, Q], F32)[:]
+                nc.vector.tensor_copy(me_listed, me[j][:].indirect(idx4[:]))
             result = sbuf(f"result{j}", [P, Q], F32)
-            nc.vector.tensor_tensor(result[:], o_bank[:], me_listed[:], MAX)
+            nc.vector.tensor_tensor(result[:], o_bank[:], me_listed, MAX)
             nc.sync.dma_start(out[j * P : (j + 1) * P, :], result[:])

@@ -125,40 +125,45 @@ def tile_attend_passedthrough_memorylarger_lean_kernel(
         nc.vector.tensor_copy(k_codes[1][:], key_words[:].indirect(list_half(idx, 1)))
 
         a_sb = sbuf("a_sb", [P, Q_TILES, I], F32)
+        a_first = [bank(f"a_first{h}", [P, half], h) for h in range(Q_TILES)]
         for h in range(Q_TILES):
-            a_first = bank(f"a_first{h}", [P, half], h)
-            product(a_first[:], q_mx[h], (k_codes[0][:], k_scales[:, 0:half]))
-            if h == 0:
-                nc.scalar.copy(a_sb[:, h, 0:half], a_first[:])
-            else:
-                nc.vector.tensor_copy(a_sb[:, h, 0:half], a_first[:])
-            nc.scalar.activation(f0[h][:].indirect(list_half(idx2, 0)), a_sb[:, h, 0:half], COPY)
-        a_second = bank("a_second", [P, Q_TILES, half], 1)
+            product(a_first[h][:], q_mx[h], (k_codes[0][:], k_scales[:, 0:half]))
+        nc.scalar.copy(a_sb[:, 0, 0:half], a_first[0][:])
+        nc.vector.tensor_copy(a_sb[:, 1, 0:half], a_first[1][:])
+        a_second = [bank(f"a_second{h}", [P, half], h) for h in range(Q_TILES)]
         for h in range(Q_TILES):
-            product(a_second[:, h, :], q_mx[h], (k_codes[1][:], k_scales[:, half:I]))
+            product(a_second[h][:], q_mx[h], (k_codes[1][:], k_scales[:, half:I]))
+        nc.scalar.activation(f0[0][:].indirect(list_half(idx2, 0)), a_sb[:, 0, 0:half], COPY)
+        nc.vector.tensor_copy(f0[1][:].indirect(list_half(idx2, 0)), a_sb[:, 1, 0:half])
+        nc.scalar.copy(a_sb[:, 0, half:I], a_second[0][:])
+        nc.vector.tensor_copy(a_sb[:, 1, half:I], a_second[1][:])
         for h in range(Q_TILES):
-            nc.scalar.copy(a_sb[:, h, half:I], a_second[:, h, :])
             nc.scalar.activation(f0[h][:].indirect(list_half(idx2, 1)), a_sb[:, h, half:I], COPY)
 
-        def round_and_quantize(name, raw):
+        def round_and_quantize(name, raw, on_gpsimd):
             width = raw.shape[2]
             grouped = sbuf(f"{name}_grouped", [P, width, PACK], BF16)
             codes = sbuf(f"{name}_codes", [P, width], U32)
             scales = sbuf(f"{name}_scales", [P, width], U8)
             pieces = [slice(0, width // 2), slice(width // 2, width)]
             for cols in pieces:
-                dst, src = interleave_views(grouped[:, cols, :], raw[:, :, cols])
-                nc.vector.tensor_copy(dst, src)
+                if on_gpsimd:
+                    nc.gpsimd.tensor_scalar(
+                        grouped[:, cols, :], raw[:, :, cols].rearrange("p t c -> p c t"), 1.0, 0.0, MULT, ADD
+                    )
+                else:
+                    dst, src = interleave_views(grouped[:, cols, :], raw[:, :, cols])
+                    nc.vector.tensor_copy(dst, src)
             for cols in pieces:
                 quantize(nc, codes[:, cols], scales[:, cols], grouped[:, cols, :].rearrange("p c t -> p (c t)"))
             return codes, scales
 
-        wm_codes, wm_scales = round_and_quantize("wm", wm_raw)
+        wm_codes, wm_scales = round_and_quantize("wm", wm_raw, True)
 
         me = [sbuf(f"me{j}", [P, M], F32) for j in range(E_TILES)]
         me_ps = []
         for h in range(M_HALVES):
-            ms_codes, ms_scales = round_and_quantize(f"ms{h}", ms_raw[h])
+            ms_codes, ms_scales = round_and_quantize(f"ms{h}", ms_raw[h], False)
             for j in range(E_TILES):
                 me_bank = bank(f"me_ps{h}{j}", [P, BANK], (2 + E_TILES * h + j) % 8)
                 cols = slice(j * P, (j + 1) * P)
@@ -178,7 +183,10 @@ def tile_attend_passedthrough_memorylarger_lean_kernel(
             for t in range(PACK):
                 nc.tensor.transpose(s_turned[h][:, t, :], s_sb[:, h, t::PACK], ident[:])
         for j in range(E_TILES):
-            nc.vector.tensor_copy(me[j][:, BANK:M], me_ps[E_TILES + j][:])
+            if j < 2:
+                nc.scalar.copy(me[j][:, BANK:M], me_ps[E_TILES + j][:])
+            else:
+                nc.vector.tensor_copy(me[j][:, BANK:M], me_ps[E_TILES + j][:])
         for h in range(Q_TILES):
             nc.vector.scalar_tensor_tensor(
                 out=w_grouped[:, h * P : (h + 1) * P, :],
@@ -191,8 +199,11 @@ def tile_attend_passedthrough_memorylarger_lean_kernel(
         quantize(nc, w_codes[:], w_scales[:], w_grouped[:].rearrange("p q t -> p (q t)"))
 
 
-        last = E_TILES - 1
-        last_listed = None
+        first_words = sbuf("first_words", [P, 2 * P], F32, tag="v_raw1")
+        middle_words = sbuf("middle_words", [P, 4 * P], F32, tag="v_raw3")
+        last_words = sbuf("last_words", [P, 2 * P], F32)
+        v_words = [first_words[:], middle_words[:, 0 : 2 * P], middle_words[:, 2 * P :], last_words[:]]
+        turned = []
         for j in range(E_TILES):
             v_listed = sbuf(f"v_listed{j}", [P, I], BF16)
             nc.scalar.activation(v_listed[:], v_raw[j][:].indirect(idx[:]), COPY)
@@ -200,22 +211,16 @@ def tile_attend_passedthrough_memorylarger_lean_kernel(
             v_turned = bank(f"v_turned{j}", [P, 2, P], 4 + j)
             for u in range(2):
                 nc.tensor.transpose(v_turned[:, u, :], pairs[:, u::2], ident[:])
-            staged = sbuf(f"staged{j}", [P, 2 * P + (Q if j == last - 1 else 0)], F32, tag=f"v_raw{j + 1}")
-            v_grouped = staged[:, 0 : 2 * P]
-            if j == last - 1:
-                last_listed = staged[:, 2 * P :]
-            nc.scalar.copy(v_grouped.rearrange("p (e u) -> p e u", u=2), v_turned[:].rearrange("p u e -> p e u"))
+            turned.append(v_turned)
+        for j in range(E_TILES):
+            nc.scalar.copy(v_words[j].rearrange("p (e u) -> p e u", u=2), turned[j][:].rearrange("p u e -> p e u"))
             v_codes = sbuf(f"v_codes{j}", [P, P], U32)
             v_scales = sbuf(f"v_scales{j}", [P, P], U8)
-            quantize(nc, v_codes[:], v_scales[:], v_grouped.bitcast(BF16))
+            quantize(nc, v_codes[:], v_scales[:], v_words[j].bitcast(BF16))
             o_bank = bank(f"o_bank{j}", [P, Q], j)
             product(o_bank[:], (v_codes[:], v_scales[:]), (w_codes[:], w_scales[:]))
-            if j == last:
-                me_listed = last_listed
-                nc.scalar.activation(me_listed, me[j][:].indirect(idx4[:]), COPY)
-            else:
-                me_listed = sbuf(f"me_listed{j}", [P, Q], F32)[:]
-                nc.vector.tensor_copy(me_listed, me[j][:].indirect(idx4[:]))
+            me_listed = sbuf(f"me_listed{j}", [P, Q], F32)
+            nc.vector.tensor_copy(me_listed[:], me[j][:].indirect(idx4[:]))
             result = sbuf(f"result{j}", [P, Q], F32)
-            nc.vector.tensor_tensor(result[:], o_bank[:], me_listed, MAX)
+            nc.vector.tensor_tensor(result[:], o_bank[:], me_listed[:], MAX)
             nc.sync.dma_start(out[j * P : (j + 1) * P, :], result[:])

@@ -15,25 +15,36 @@ MAX = mybir.AluOpType.max
 MULT = mybir.AluOpType.mult
 ADD = mybir.AluOpType.add
 
+D, T, I, Q, E, Z, M, C = 512, 2048, 512, 256, 512, 1024, 1024, 512
+FLOPS = 2 * (D * I * Q + I * E * Q + C * E * M)
+
 P = 128
 PACK = 4
-D, T, I, Q, E, Z, M, C = 512, 2048, 512, 256, 512, 1024, 1024, 512
+QUADRANT = 32
+SCALE_ROWS = 4
+PER_COLUMN = 16
 BANK = 512
+N_BANKS = 8
 Q_TILES = Q // P
 E_TILES = E // P
 M_HALVES = M // BANK
-FLOPS = 2 * (D * I * Q + I * E * Q + C * E * M)
+HALF = I // 2
+PAIRS = PACK // 2
+RUN = 4
+ME_COPIES_ON_SCALAR = 2
+EARLY_LOOKUPS = 2
 
 
 def interleave_views(grouped, raw):
     return (
-        grouped.rearrange("p (c i) t -> p c t i", i=4),
-        raw.rearrange("p t (c i) -> p c t i", i=4),
+        grouped.rearrange("p (c i) t -> p c t i", i=RUN),
+        raw.rearrange("p t (c i) -> p c t i", i=RUN),
     )
 
 
-def quantize(nc, codes, scales, grouped):
-    nc.vector.quantize_mx(out=codes.bitcast(FP8X4), scales=scales, in_=grouped)
+def list_half(offsets, part):
+    columns = HALF // PER_COLUMN
+    return offsets[:, part * columns : (part + 1) * columns]
 
 
 def tile_attend_passedthrough_memorylarger_lean_kernel(
@@ -44,15 +55,18 @@ def tile_attend_passedthrough_memorylarger_lean_kernel(
         sb = ctx.enter_context(tc.tile_pool(name="sb", bufs=1))
         ps = ctx.enter_context(tc.psum_pool(name="ps", bufs=1))
 
-        def sbuf(name, shape, dtype, tag=None):
-            return sb.tile(shape, dtype, name=name, tag=tag or name, align_bytes=64)
+        def sbuf(name, shape, dtype, reuse=None):
+            return sb.tile(shape, dtype, name=name, tag=reuse or name, align_bytes=64)
 
         def bank(name, shape, number):
             return ps.tile(shape, F32, name=name, tag=f"bank{number}")
 
-        def product(out_ap, stationary, moving):
+        def quantize(codes, scales, grouped):
+            nc.vector.quantize_mx(out=codes.bitcast(FP8X4), scales=scales, in_=grouped)
+
+        def product(result, stationary, moving):
             nc.tensor.matmul_mx(
-                out=out_ap,
+                out=result,
                 lhsT=stationary[0].bitcast(FP8X4),
                 lhsT_scale=stationary[1],
                 rhs=moving[0].bitcast(FP8X4),
@@ -61,15 +75,33 @@ def tile_attend_passedthrough_memorylarger_lean_kernel(
                 stop=True,
             )
 
-        idx = sbuf("idx", [P, I // 16], U16)
-        idx2 = sbuf("idx2", [P, I // 16], U16)
-        idx3 = sbuf("idx3", [P, I // 16], U16)
-        idx4 = sbuf("idx4", [P, Q // 16], U16)
+        def round_on_vector(grouped, raw):
+            nc.vector.tensor_copy(*interleave_views(grouped, raw))
+
+        def round_on_gpsimd(grouped, raw):
+            nc.gpsimd.tensor_scalar(grouped, raw.rearrange("p t c -> p c t"), 1.0, 0.0, MULT, ADD)
+
+        def round_and_quantize(name, raw, round_piece):
+            width = raw.shape[2]
+            grouped = sbuf(f"{name}_grouped", [P, width, PACK], BF16)
+            codes = sbuf(f"{name}_codes", [P, width], U32)
+            scales = sbuf(f"{name}_scales", [P, width], U8)
+            pieces = [slice(0, width // 2), slice(width // 2, width)]
+            for cols in pieces:
+                round_piece(grouped[:, cols, :], raw[:, :, cols])
+            for cols in pieces:
+                quantize(codes[:, cols], scales[:, cols], grouped[:, cols, :].rearrange("p c t -> p (c t)"))
+            return codes, scales
+
+        idx = sbuf("idx", [P, I // PER_COLUMN], U16)
+        idx2 = sbuf("idx2", [P, I // PER_COLUMN], U16)
+        idx3 = sbuf("idx3", [P, I // PER_COLUMN], U16)
+        idx4 = sbuf("idx4", [P, Q // PER_COLUMN], U16)
         key_words = sbuf("key_words", [P, T], U32)
         key_scales = sbuf("key_scales", [P, T], U8)
         q_raw = sbuf("q_raw", [P, PACK, Q], F32)
         wm_raw = sbuf("wm_raw", [P, PACK, E], F32)
-        ms_raw = [sbuf(f"ms_raw{h}", [P, PACK, BANK], F32, tag=f"ms_raw{h}") for h in range(M_HALVES)]
+        ms_raw = [sbuf(f"ms_raw{half}", [P, PACK, BANK], F32) for half in range(M_HALVES)]
         v_raw = [sbuf(f"v_raw{j}", [P, T], F32) for j in range(E_TILES)]
         factor = sbuf("factor", [P, PACK], F32)
         f0 = [sbuf(f"f0_{h}", [P, Z], F32) for h in range(Q_TILES)]
@@ -78,10 +110,10 @@ def tile_attend_passedthrough_memorylarger_lean_kernel(
         nc.gpsimd.memset(key_scales[:].bitcast(I32), 0)
         nc.sync.dma_start(q_raw[:], query.rearrange("(p t) q -> p t q", t=PACK))
         nc.sync.dma_start(idx[:], offs)
-        for quad in range(4):
+        for quad in range(P // QUADRANT):
             nc.sync.dma_start(
-                key_scales[32 * quad : 32 * quad + 4, :].bitcast(I32),
-                keys_scales[0, 4 * quad : 4 * quad + 4, :].bitcast(I32),
+                key_scales[QUADRANT * quad : QUADRANT * quad + SCALE_ROWS, :].bitcast(I32),
+                keys_scales[0, SCALE_ROWS * quad : SCALE_ROWS * (quad + 1), :].bitcast(I32),
             )
         nc.sync.dma_start(
             key_words[:].bitcast(I32), keys_words[0].rearrange("p n t -> p (n t)").bitcast(I32)
@@ -91,9 +123,9 @@ def tile_attend_passedthrough_memorylarger_lean_kernel(
         nc.sync.dma_start(idx3[:], offs3)
         nc.sync.dma_start(idx4[:], offs4)
         nc.sync.dma_start(factor[:], slot_factor.rearrange("o (p t) -> (o p) t", t=PACK))
-        ms_view = mstore.rearrange("(p t) m -> p t m", t=PACK)
-        for h in range(M_HALVES):
-            nc.sync.dma_start(ms_raw[h][:], ms_view[:, :, h * BANK : (h + 1) * BANK])
+        ms_rows = mstore.rearrange("(p t) m -> p t m", t=PACK)
+        for half in range(M_HALVES):
+            nc.sync.dma_start(ms_raw[half][:], ms_rows[:, :, half * BANK : (half + 1) * BANK])
         for j in range(E_TILES):
             nc.sync.dma_start(v_raw[j][:], vals[j * P : (j + 1) * P, :])
 
@@ -101,15 +133,9 @@ def tile_attend_passedthrough_memorylarger_lean_kernel(
             nc.vector.memset(f0[h][:], 0.0)
         make_identity(nc, ident[:])
 
-        half = I // 2
-
-        def list_half(offsets, part):
-            return offsets[:, part * (half // 16) : (part + 1) * (half // 16)]
-
         k_scales = sbuf("k_scales", [P, I], U8)
+        k_codes = [sbuf(f"k_codes{part}", [P, HALF], U32) for part in range(2)]
         nc.vector.tensor_copy(k_scales[:], key_scales[:].indirect(idx[:]))
-        k_codes = [None, None]
-        k_codes[0] = sbuf("k_codes0", [P, half], U32)
         nc.vector.tensor_copy(k_codes[0][:], key_words[:].indirect(list_half(idx, 0)))
 
         q_mx = []
@@ -117,76 +143,61 @@ def tile_attend_passedthrough_memorylarger_lean_kernel(
             q_grouped = sbuf(f"q_grouped{h}", [P, P, PACK], BF16)
             q_codes = sbuf(f"q_codes{h}", [P, P], U32)
             q_scales = sbuf(f"q_scales{h}", [P, P], U8)
-            dst, src = interleave_views(q_grouped[:], q_raw[:, :, h * P : (h + 1) * P])
-            nc.scalar.activation(dst, src, COPY)
-            quantize(nc, q_codes[:], q_scales[:], q_grouped[:].rearrange("p q t -> p (q t)"))
+            nc.scalar.activation(*interleave_views(q_grouped[:], q_raw[:, :, h * P : (h + 1) * P]), COPY)
+            quantize(q_codes[:], q_scales[:], q_grouped[:].rearrange("p q t -> p (q t)"))
             q_mx.append((q_codes[:], q_scales[:]))
-        k_codes[1] = sbuf("k_codes1", [P, half], U32)
         nc.vector.tensor_copy(k_codes[1][:], key_words[:].indirect(list_half(idx, 1)))
 
         a_sb = sbuf("a_sb", [P, Q_TILES, I], F32)
-        a_first = [bank(f"a_first{h}", [P, half], h) for h in range(Q_TILES)]
+        a_first = [bank(f"a_first{h}", [P, HALF], h) for h in range(Q_TILES)]
         for h in range(Q_TILES):
-            product(a_first[h][:], q_mx[h], (k_codes[0][:], k_scales[:, 0:half]))
-        nc.scalar.copy(a_sb[:, 0, 0:half], a_first[0][:])
-        nc.vector.tensor_copy(a_sb[:, 1, 0:half], a_first[1][:])
-        a_second = [bank(f"a_second{h}", [P, half], h) for h in range(Q_TILES)]
+            product(a_first[h][:], q_mx[h], (k_codes[0][:], k_scales[:, 0:HALF]))
+        nc.scalar.copy(a_sb[:, 0, 0:HALF], a_first[0][:])
+        nc.vector.tensor_copy(a_sb[:, 1, 0:HALF], a_first[1][:])
+        a_second = [bank(f"a_second{h}", [P, HALF], h) for h in range(Q_TILES)]
         for h in range(Q_TILES):
-            product(a_second[h][:], q_mx[h], (k_codes[1][:], k_scales[:, half:I]))
-        nc.scalar.activation(f0[0][:].indirect(list_half(idx2, 0)), a_sb[:, 0, 0:half], COPY)
-        nc.vector.tensor_copy(f0[1][:].indirect(list_half(idx2, 0)), a_sb[:, 1, 0:half])
-        nc.scalar.copy(a_sb[:, 0, half:I], a_second[0][:])
-        nc.vector.tensor_copy(a_sb[:, 1, half:I], a_second[1][:])
+            product(a_second[h][:], q_mx[h], (k_codes[1][:], k_scales[:, HALF:I]))
+        nc.scalar.activation(f0[0][:].indirect(list_half(idx2, 0)), a_sb[:, 0, 0:HALF], COPY)
+        nc.vector.tensor_copy(f0[1][:].indirect(list_half(idx2, 0)), a_sb[:, 1, 0:HALF])
+        nc.scalar.copy(a_sb[:, 0, HALF:I], a_second[0][:])
+        nc.vector.tensor_copy(a_sb[:, 1, HALF:I], a_second[1][:])
         for h in range(Q_TILES):
-            nc.scalar.activation(f0[h][:].indirect(list_half(idx2, 1)), a_sb[:, h, half:I], COPY)
+            nc.scalar.activation(f0[h][:].indirect(list_half(idx2, 1)), a_sb[:, h, HALF:I], COPY)
 
-        def round_and_quantize(name, raw, on_gpsimd):
-            width = raw.shape[2]
-            grouped = sbuf(f"{name}_grouped", [P, width, PACK], BF16)
-            codes = sbuf(f"{name}_codes", [P, width], U32)
-            scales = sbuf(f"{name}_scales", [P, width], U8)
-            pieces = [slice(0, width // 2), slice(width // 2, width)]
-            for cols in pieces:
-                if on_gpsimd:
-                    nc.gpsimd.tensor_scalar(
-                        grouped[:, cols, :], raw[:, :, cols].rearrange("p t c -> p c t"), 1.0, 0.0, MULT, ADD
-                    )
-                else:
-                    dst, src = interleave_views(grouped[:, cols, :], raw[:, :, cols])
-                    nc.vector.tensor_copy(dst, src)
-            for cols in pieces:
-                quantize(nc, codes[:, cols], scales[:, cols], grouped[:, cols, :].rearrange("p c t -> p (c t)"))
-            return codes, scales
-
-        wm_codes, wm_scales = round_and_quantize("wm", wm_raw, True)
-
+        wm_codes, wm_scales = round_and_quantize("wm", wm_raw, round_on_gpsimd)
         me = [sbuf(f"me{j}", [P, M], F32) for j in range(E_TILES)]
-        me_ps = []
-        for h in range(M_HALVES):
-            ms_codes, ms_scales = round_and_quantize(f"ms{h}", ms_raw[h], False)
+        me_banks = []
+        for half in range(M_HALVES):
+            ms_codes, ms_scales = round_and_quantize(f"ms{half}", ms_raw[half], round_on_vector)
             for j in range(E_TILES):
-                me_bank = bank(f"me_ps{h}{j}", [P, BANK], (2 + E_TILES * h + j) % 8)
+                me_bank = bank(f"me_bank{half}{j}", [P, BANK], (Q_TILES + E_TILES * half + j) % N_BANKS)
                 cols = slice(j * P, (j + 1) * P)
                 product(me_bank[:], (wm_codes[:, cols], wm_scales[:, cols]), (ms_codes[:], ms_scales[:]))
-                me_ps.append(me_bank)
+                me_banks.append(me_bank)
         for j in range(E_TILES):
-            nc.scalar.copy(me[j][:, 0:BANK], me_ps[j][:])
+            nc.scalar.copy(me[j][:, 0:BANK], me_banks[j][:])
 
         w_grouped = sbuf("w_grouped", [P, Q, PACK], BF16)
         w_codes = sbuf("w_codes", [P, Q], U32)
         w_scales = sbuf("w_scales", [P, Q], U8)
-        s_sb = sbuf("s_sb", [P, Q_TILES, I], F32, tag="ms1_grouped")
+        s_sb = sbuf("s_sb", [P, Q_TILES, I], F32, reuse=f"ms{M_HALVES - 1}_grouped")
         s_turned = []
         for h in range(Q_TILES):
             nc.vector.tensor_tensor(s_sb[:, h, :], f0[h][:].indirect(idx3[:]), a_sb[:, h, :], ADD)
-            s_turned.append(bank(f"s_turned{h}", [P, PACK, P], 2 + h))
+            s_turned.append(bank(f"s_turned{h}", [P, PACK, P], Q_TILES + h))
             for t in range(PACK):
                 nc.tensor.transpose(s_turned[h][:, t, :], s_sb[:, h, t::PACK], ident[:])
+
         for j in range(E_TILES):
-            if j < 2:
-                nc.scalar.copy(me[j][:, BANK:M], me_ps[E_TILES + j][:])
+            if j < ME_COPIES_ON_SCALAR:
+                nc.scalar.copy(me[j][:, BANK:M], me_banks[E_TILES + j][:])
             else:
-                nc.vector.tensor_copy(me[j][:, BANK:M], me_ps[E_TILES + j][:])
+                nc.vector.tensor_copy(me[j][:, BANK:M], me_banks[E_TILES + j][:])
+        last = E_TILES - 1
+        me_listed = [sbuf(f"me_listed{j}", [P, Q], F32) for j in range(last)]
+        for j in range(EARLY_LOOKUPS):
+            nc.vector.tensor_copy(me_listed[j][:], me[j][:].indirect(idx4[:]))
+
         for h in range(Q_TILES):
             nc.vector.scalar_tensor_tensor(
                 out=w_grouped[:, h * P : (h + 1) * P, :],
@@ -196,31 +207,36 @@ def tile_attend_passedthrough_memorylarger_lean_kernel(
                 op0=MAX,
                 op1=MULT,
             )
-        quantize(nc, w_codes[:], w_scales[:], w_grouped[:].rearrange("p q t -> p (q t)"))
+        quantize(w_codes[:], w_scales[:], w_grouped[:].rearrange("p q t -> p (q t)"))
 
-
-        first_words = sbuf("first_words", [P, 2 * P], F32, tag="v_raw1")
-        middle_words = sbuf("middle_words", [P, 4 * P], F32, tag="v_raw3")
-        last_words = sbuf("last_words", [P, 2 * P], F32)
-        v_words = [first_words[:], middle_words[:, 0 : 2 * P], middle_words[:, 2 * P :], last_words[:]]
-        turned = []
+        words = PAIRS * P
+        first_words = sbuf("first_words", [P, words], F32, reuse="v_raw1")
+        middle_words = sbuf("middle_words", [P, 2 * words], F32, reuse=f"v_raw{last}")
+        last_words = sbuf("last_words", [P, words], F32)
+        v_words = [first_words[:], middle_words[:, 0:words], middle_words[:, words:], last_words[:]]
+        v_turned = []
         for j in range(E_TILES):
             v_listed = sbuf(f"v_listed{j}", [P, I], BF16)
             nc.scalar.activation(v_listed[:], v_raw[j][:].indirect(idx[:]), COPY)
             pairs = v_listed[:].bitcast(F32)
-            v_turned = bank(f"v_turned{j}", [P, 2, P], 4 + j)
-            for u in range(2):
-                nc.tensor.transpose(v_turned[:, u, :], pairs[:, u::2], ident[:])
-            turned.append(v_turned)
+            v_turned.append(bank(f"v_turned{j}", [P, PAIRS, P], N_BANKS - E_TILES + j))
+            for u in range(PAIRS):
+                nc.tensor.transpose(v_turned[j][:, u, :], pairs[:, u::PAIRS], ident[:])
+
         for j in range(E_TILES):
-            nc.scalar.copy(v_words[j].rearrange("p (e u) -> p e u", u=2), turned[j][:].rearrange("p u e -> p e u"))
+            nc.scalar.copy(
+                v_words[j].rearrange("p (e u) -> p e u", u=PAIRS), v_turned[j][:].rearrange("p u e -> p e u")
+            )
             v_codes = sbuf(f"v_codes{j}", [P, P], U32)
             v_scales = sbuf(f"v_scales{j}", [P, P], U8)
-            quantize(nc, v_codes[:], v_scales[:], v_words[j].bitcast(BF16))
+            quantize(v_codes[:], v_scales[:], v_words[j].bitcast(BF16))
             o_bank = bank(f"o_bank{j}", [P, Q], j)
             product(o_bank[:], (v_codes[:], v_scales[:]), (w_codes[:], w_scales[:]))
-            me_listed = sbuf(f"me_listed{j}", [P, Q], F32)
-            nc.vector.tensor_copy(me_listed[:], me[j][:].indirect(idx4[:]))
+            if j == last:
+                me_listed.append(sbuf(f"me_listed{j}", [P, Q], F32, reuse=f"v_listed{j}"))
+                nc.scalar.activation(me_listed[j][:], me[j][:].indirect(idx4[:]), COPY)
+            elif j >= EARLY_LOOKUPS:
+                nc.vector.tensor_copy(me_listed[j][:], me[j][:].indirect(idx4[:]))
             result = sbuf(f"result{j}", [P, Q], F32)
-            nc.vector.tensor_tensor(result[:], o_bank[:], me_listed[:], MAX)
+            nc.vector.tensor_tensor(result[:], o_bank[:], me_listed[j][:], MAX)
             nc.sync.dma_start(out[j * P : (j + 1) * P, :], result[:])

from contextlib import ExitStack

import concourse.mybir as mybir
from concourse.masks import make_identity

F32 = mybir.dt.float32
BF16 = mybir.dt.bfloat16
I32 = mybir.dt.int32
U32 = mybir.dt.uint32
U16 = mybir.dt.uint16
U8 = mybir.dt.uint8
FP8X4 = mybir.dt.float8_e4m3fn_x4
COPY = mybir.ActivationFunctionType.Copy
MAX = mybir.AluOpType.max
MULT = mybir.AluOpType.mult
ADD = mybir.AluOpType.add

D, T, I, Q, E, Z, M, C = 512, 2048, 512, 256, 512, 1024, 1024, 512
FLOPS = 2 * (D * I * Q + I * E * Q + C * E * M)

P = 128
PACK = 4
QUADRANT = 32
SCALE_ROWS = 4
PER_COLUMN = 16
BANK = 512
N_BANKS = 8
Q_TILES = Q // P
E_TILES = E // P
M_HALVES = M // BANK
HALF = I // 2
PAIRS = PACK // 2
RUN = 4
ME_COPIES_ON_SCALAR = 2
EARLY_LOOKUPS = 2


def interleave_views(grouped, raw):
    return (
        grouped.rearrange("p (c i) t -> p c t i", i=RUN),
        raw.rearrange("p t (c i) -> p c t i", i=RUN),
    )


def list_half(offsets, part):
    columns = HALF // PER_COLUMN
    return offsets[:, part * columns : (part + 1) * columns]


def tile_attend_passedthrough_memorylarger_lean_kernel(
    tc, query, keys_words, keys_scales, slot_factor, vals, wm, mstore, offs, offs2, offs3, offs4, out
):
    nc = tc.nc
    with ExitStack() as ctx:
        sb = ctx.enter_context(tc.tile_pool(name="sb", bufs=1))
        ps = ctx.enter_context(tc.psum_pool(name="ps", bufs=1))

        def sbuf(name, shape, dtype, reuse=None):
            return sb.tile(shape, dtype, name=name, tag=reuse or name, align_bytes=64)

        def bank(name, shape, number):
            return ps.tile(shape, F32, name=name, tag=f"bank{number}")

        def quantize(codes, scales, grouped):
            nc.vector.quantize_mx(out=codes.bitcast(FP8X4), scales=scales, in_=grouped)

        def product(result, stationary, moving):
            nc.tensor.matmul_mx(
                out=result,
                lhsT=stationary[0].bitcast(FP8X4),
                lhsT_scale=stationary[1],
                rhs=moving[0].bitcast(FP8X4),
                rhs_scale=moving[1],
                start=True,
                stop=True,
            )

        def round_on_vector(grouped, raw):
            nc.vector.tensor_copy(*interleave_views(grouped, raw))

        def round_on_gpsimd(grouped, raw):
            nc.gpsimd.tensor_scalar(grouped, raw.rearrange("p t c -> p c t"), 1.0, 0.0, MULT, ADD)

        def round_and_quantize(name, raw, round_piece):
            width = raw.shape[2]
            grouped = sbuf(f"{name}_grouped", [P, width, PACK], BF16)
            codes = sbuf(f"{name}_codes", [P, width], U32)
            scales = sbuf(f"{name}_scales", [P, width], U8)
            pieces = [slice(0, width // 2), slice(width // 2, width)]
            for cols in pieces:
                round_piece(grouped[:, cols, :], raw[:, :, cols])
            for cols in pieces:
                quantize(codes[:, cols], scales[:, cols], grouped[:, cols, :].rearrange("p c t -> p (c t)"))
            return codes, scales

        idx = sbuf("idx", [P, I // PER_COLUMN], U16)
        idx2 = sbuf("idx2", [P, I // PER_COLUMN], U16)
        idx3 = sbuf("idx3", [P, I // PER_COLUMN], U16)
        idx4 = sbuf("idx4", [P, Q // PER_COLUMN], U16)
        key_words = sbuf("key_words", [P, T], U32)
        key_scales = sbuf("key_scales", [P, T], U8)
        q_raw = sbuf("q_raw", [P, PACK, Q], F32)
        wm_raw = sbuf("wm_raw", [P, PACK, E], F32)
        ms_raw = [sbuf(f"ms_raw{half}", [P, PACK, BANK], F32) for half in range(M_HALVES)]
        v_raw = [sbuf(f"v_raw{j}", [P, T], F32) for j in range(E_TILES)]
        factor = sbuf("factor", [P, PACK], F32)
        f0 = [sbuf(f"f0_{h}", [P, Z], F32) for h in range(Q_TILES)]
        ident = sbuf("ident", [P, P], F32)

        nc.gpsimd.memset(key_scales[:].bitcast(I32), 0)
        nc.sync.dma_start(q_raw[:], query.rearrange("(p t) q -> p t q", t=PACK))
        nc.sync.dma_start(idx[:], offs)
        for quad in range(P // QUADRANT):
            nc.sync.dma_start(
                key_scales[QUADRANT * quad : QUADRANT * quad + SCALE_ROWS, :].bitcast(I32),
                keys_scales[0, SCALE_ROWS * quad : SCALE_ROWS * (quad + 1), :].bitcast(I32),
            )
        nc.sync.dma_start(
            key_words[:].bitcast(I32), keys_words[0].rearrange("p n t -> p (n t)").bitcast(I32)
        )
        nc.sync.dma_start(idx2[:], offs2)
        nc.sync.dma_start(wm_raw[:], wm.rearrange("(p t) e -> p t e", t=PACK))
        nc.sync.dma_start(idx3[:], offs3)
        nc.sync.dma_start(idx4[:], offs4)
        nc.sync.dma_start(factor[:], slot_factor.rearrange("o (p t) -> (o p) t", t=PACK))
        ms_rows = mstore.rearrange("(p t) m -> p t m", t=PACK)
        for half in range(M_HALVES):
            nc.sync.dma_start(ms_raw[half][:], ms_rows[:, :, half * BANK : (half + 1) * BANK])
        for j in range(E_TILES):
            nc.sync.dma_start(v_raw[j][:], vals[j * P : (j + 1) * P, :])

        for h in range(Q_TILES):
            nc.vector.memset(f0[h][:], 0.0)
        make_identity(nc, ident[:])

        k_scales = sbuf("k_scales", [P, I], U8)
        k_codes = [sbuf(f"k_codes{part}", [P, HALF], U32) for part in range(2)]
        nc.vector.tensor_copy(k_scales[:], key_scales[:].indirect(idx[:]))
        nc.vector.tensor_copy(k_codes[0][:], key_words[:].indirect(list_half(idx, 0)))

        q_mx = []
        for h in range(Q_TILES):
            q_grouped = sbuf(f"q_grouped{h}", [P, P, PACK], BF16)
            q_codes = sbuf(f"q_codes{h}", [P, P], U32)
            q_scales = sbuf(f"q_scales{h}", [P, P], U8)
            nc.scalar.activation(*interleave_views(q_grouped[:], q_raw[:, :, h * P : (h + 1) * P]), COPY)
            quantize(q_codes[:], q_scales[:], q_grouped[:].rearrange("p q t -> p (q t)"))
            q_mx.append((q_codes[:], q_scales[:]))
        nc.vector.tensor_copy(k_codes[1][:], key_words[:].indirect(list_half(idx, 1)))

        a_sb = sbuf("a_sb", [P, Q_TILES, I], F32)
        a_first = [bank(f"a_first{h}", [P, HALF], h) for h in range(Q_TILES)]
        for h in range(Q_TILES):
            product(a_first[h][:], q_mx[h], (k_codes[0][:], k_scales[:, 0:HALF]))
        nc.scalar.copy(a_sb[:, 0, 0:HALF], a_first[0][:])
        nc.vector.tensor_copy(a_sb[:, 1, 0:HALF], a_first[1][:])
        a_second = [bank(f"a_second{h}", [P, HALF], h) for h in range(Q_TILES)]
        for h in range(Q_TILES):
            product(a_second[h][:], q_mx[h], (k_codes[1][:], k_scales[:, HALF:I]))
        nc.scalar.activation(f0[0][:].indirect(list_half(idx2, 0)), a_sb[:, 0, 0:HALF], COPY)
        nc.vector.tensor_copy(f0[1][:].indirect(list_half(idx2, 0)), a_sb[:, 1, 0:HALF])
        nc.scalar.copy(a_sb[:, 0, HALF:I], a_second[0][:])
        nc.vector.tensor_copy(a_sb[:, 1, HALF:I], a_second[1][:])
        for h in range(Q_TILES):
            nc.scalar.activation(f0[h][:].indirect(list_half(idx2, 1)), a_sb[:, h, HALF:I], COPY)

        wm_codes, wm_scales = round_and_quantize("wm", wm_raw, round_on_gpsimd)
        me = [sbuf(f"me{j}", [P, M], F32) for j in range(E_TILES)]
        me_banks = []
        for half in range(M_HALVES):
            ms_codes, ms_scales = round_and_quantize(f"ms{half}", ms_raw[half], round_on_vector)
            for j in range(E_TILES):
                me_bank = bank(f"me_bank{half}{j}", [P, BANK], (Q_TILES + E_TILES * half + j) % N_BANKS)
                cols = slice(j * P, (j + 1) * P)
                product(me_bank[:], (wm_codes[:, cols], wm_scales[:, cols]), (ms_codes[:], ms_scales[:]))
                me_banks.append(me_bank)
        for j in range(E_TILES):
            nc.scalar.copy(me[j][:, 0:BANK], me_banks[j][:])

        w_grouped = sbuf("w_grouped", [P, Q, PACK], BF16)
        w_codes = sbuf("w_codes", [P, Q], U32)
        w_scales = sbuf("w_scales", [P, Q], U8)
        s_sb = sbuf("s_sb", [P, Q_TILES, I], F32, reuse=f"ms{M_HALVES - 1}_grouped")
        s_turned = []
        for h in range(Q_TILES):
            nc.vector.tensor_tensor(s_sb[:, h, :], f0[h][:].indirect(idx3[:]), a_sb[:, h, :], ADD)
            s_turned.append(bank(f"s_turned{h}", [P, PACK, P], Q_TILES + h))
            for t in range(PACK):
                nc.tensor.transpose(s_turned[h][:, t, :], s_sb[:, h, t::PACK], ident[:])

        for j in range(E_TILES):
            if j < ME_COPIES_ON_SCALAR:
                nc.scalar.copy(me[j][:, BANK:M], me_banks[E_TILES + j][:])
            else:
                nc.vector.tensor_copy(me[j][:, BANK:M], me_banks[E_TILES + j][:])
        last = E_TILES - 1
        me_listed = [sbuf(f"me_listed{j}", [P, Q], F32) for j in range(last)]
        for j in range(EARLY_LOOKUPS):
            nc.vector.tensor_copy(me_listed[j][:], me[j][:].indirect(idx4[:]))

        for h in range(Q_TILES):
            nc.vector.scalar_tensor_tensor(
                out=w_grouped[:, h * P : (h + 1) * P, :],
                in0=s_turned[h][:].rearrange("p t q -> p q t"),
                scalar=0.0,
                in1=factor[:].unsqueeze(1).to_broadcast([P, P, PACK]),
                op0=MAX,
                op1=MULT,
            )
        quantize(w_codes[:], w_scales[:], w_grouped[:].rearrange("p q t -> p (q t)"))

        words = PAIRS * P
        first_words = sbuf("first_words", [P, words], F32, reuse="v_raw1")
        middle_words = sbuf("middle_words", [P, 2 * words], F32, reuse=f"v_raw{last}")
        last_words = sbuf("last_words", [P, words], F32)
        v_words = [first_words[:], middle_words[:, 0:words], middle_words[:, words:], last_words[:]]
        v_turned = []
        for j in range(E_TILES):
            v_listed = sbuf(f"v_listed{j}", [P, I], BF16)
            nc.scalar.activation(v_listed[:], v_raw[j][:].indirect(idx[:]), COPY)
            pairs = v_listed[:].bitcast(F32)
            v_turned.append(bank(f"v_turned{j}", [P, PAIRS, P], N_BANKS - E_TILES + j))
            for u in range(PAIRS):
                nc.tensor.transpose(v_turned[j][:, u, :], pairs[:, u::PAIRS], ident[:])

        for j in range(E_TILES):
            nc.scalar.copy(
                v_words[j].rearrange("p (e u) -> p e u", u=PAIRS), v_turned[j][:].rearrange("p u e -> p e u")
            )
            v_codes = sbuf(f"v_codes{j}", [P, P], U32)
            v_scales = sbuf(f"v_scales{j}", [P, P], U8)
            quantize(v_codes[:], v_scales[:], v_words[j].bitcast(BF16))
            o_bank = bank(f"o_bank{j}", [P, Q], j)
            product(o_bank[:], (v_codes[:], v_scales[:]), (w_codes[:], w_scales[:]))
            if j == last:
                me_listed.append(sbuf(f"me_listed{j}", [P, Q], F32, reuse=f"v_listed{j}"))
                nc.scalar.activation(me_listed[j][:], me[j][:].indirect(idx4[:]), COPY)
            elif j >= EARLY_LOOKUPS:
                nc.vector.tensor_copy(me_listed[j][:], me[j][:].indirect(idx4[:]))
            result = sbuf(f"result{j}", [P, Q], F32)
            nc.vector.tensor_tensor(result[:], o_bank[:], me_listed[j][:], MAX)
            nc.sync.dma_start(out[j * P : (j + 1) * P, :], result[:])
